import numpy as np
CORES = [5,13,21,29,37,45,53,61,197,205,213,221,229,237,245,253]
N = 16
WIDTHS = [256,256,256,256,64,256,256,64,256,256,128,128,256,256,256,128]
XW = 256
def setup_inputs(rng):
    return {"x": rng.standard_normal((N, 128, XW), dtype=np.float32)}
def reference(x):
    g = np.concatenate([x[r][:, :WIDTHS[r]] for r in range(N)], axis=1)
    return {"y": np.broadcast_to(g, (N,) + g.shape)}

@@ -1,0 +1,77 @@
+from concourse.bass import DstId, RemoteDMATransfer
+
+SCRATCH = {
+    "land": ("sbuf", [128, 3328], "float32"),
+}
+SEMAPHORES = ["ld", "st", "arr", "own", "sent"]
+
+RANK_LANE = 5
+HELPER = (6, 2)
+OFF = 0x00FF
+HI = 0xFF00
+
+
+def rank_program(g, core, T, topo):
+    widths = T.tables["WIDTHS"]
+    cores = T.cores
+    n = len(cores)
+    base = core - core % 8
+    lane = core % 8
+    r = T.rank_of(base + RANK_LANE)
+    if r is None or (lane != RANK_LANE and lane not in HELPER):
+        return
+    off = [sum(widths[:i]) for i in range(n)]
+
+    def piece(s, k):
+        h = widths[s] // 2
+        a = off[s] + k * h
+        return T.land[:, a:a + h]
+
+    def did(dst):
+        rid, pid = topo.addr(dst, core)
+        return DstId(rid=rid, pnc=pid)
+
+    def helper(s, k):
+        return cores[s] - RANK_LANE + HELPER[k]
+
+    def send(ap, dsts, mask, sem):
+        return RemoteDMATransfer(dst_ids=[did(d) for d in dsts], dma_engine_mask=mask, remote_sem=sem,
+                                 srcs=[ap], dsts=[ap for d in dsts])
+
+    me = cores[r]
+    peers = [s for s in range(n) if topo.same_plane(cores[s], me)]
+    mate = [s for s in range(n) if topo.mates(cores[s], me)][0]
+    S = T.sem
+
+    if lane == RANK_LANE:
+        g.dma_start(T.land[:, off[r]:off[r] + widths[r]], T.x[:, 0:widths[r]]).then_inc(S.ld, 16)
+        g.wait_ge(S.ld, 16)
+        g.remote_dma_fused([
+            send(piece(r, 0), [helper(s, 0) for s in peers + [r]], OFF, S.arr),
+            send(piece(r, 1), [helper(r, 1)], HI, S.own),
+        ], local_sem=S.sent)
+        g.wait_ge(S.sent, 16)
+        g.wait_ge(S.arr, 8 * (4 * len(peers) + 2))
+        g.dma_start(T.y[:, :], T.land[:, :]).then_inc(S.st, 16)
+        g.wait_ge(S.st, 16)
+        return
+
+    k = HELPER.index(lane)
+    sent = 0
+    if k == 1:
+        g.wait_ge(S.own, 8)
+        g.remote_dma_fused([send(piece(r, 1), [helper(s, 1) for s in peers] + [cores[mate]], OFF, S.arr)],
+                           local_sem=S.sent)
+        sent += 8
+        g.wait_ge(S.arr, 8 * len(peers))
+    else:
+        g.wait_ge(S.arr, 8 * (len(peers) + 1))
+        g.remote_dma_fused([send(piece(r, 0), [cores[mate]], OFF, S.arr)], local_sem=S.sent)
+        sent += 8
+    for s in peers:
+        g.remote_dma_fused([
+            send(piece(s, k), [cores[mate]], OFF, S.arr),
+            send(piece(s, k), [me], HI, S.arr),
+        ], local_sem=S.sent)
+        sent += 16
+    g.wait_ge(S.sent, sent)

@@ -2,76 +2,125 @@ from concourse.bass import DstId, RemoteDMATransfer
 
 SCRATCH = {
     "land": ("sbuf", [128, 3328], "float32"),
+    "d256": ("dram", [2, 128, 256], "float32"),
+    "d128": ("dram", [2, 128, 128], "float32"),
+    "d64": ("dram", [2, 128, 64], "float32"),
+    "h128": ("dram", [2, 128, 128], "float32"),
 }
-SEMAPHORES = ["ld", "st", "arr", "own", "sent"]
+SEMAPHORES = ["ld", "st", "arr0", "arr1", "blk0", "blk1", "half", "sent"]
 
 RANK_LANE = 5
-HELPER = (6, 2)
-OFF = 0x00FF
-HI = 0xFF00
+DISTRIBUTOR = (4, 0)
+FORWARDER = (6, 2, 3, 7)
+ALL, OFF, HI = 0xFFFF, 0x00FF, 0xFF00
+
+
+def plan(widths, cores, topo):
+    n = len(cores)
+    planes, lane, slot = {}, {}, {}
+    for first in (0, 1):
+        pl = [s for s in range(n) if s == first or topo.same_plane(cores[s], cores[first])]
+        low = sorted([s for s in pl if s < n // 2], key=lambda s: -widths[s])
+        high = sorted([s for s in pl if s >= n // 2], key=lambda s: widths[s])
+        pairs = sorted(zip(low, high), key=lambda p: -(widths[p[0]] + widths[p[1]]))
+        for i, p in enumerate(pairs):
+            for j in (0, 1):
+                lane[p[j]], slot[p[j]], planes[p[j]] = FORWARDER[i], j, pl
+    return planes, lane, slot
+
+
+def way(s, d, planes, widths):
+    pl = planes[s]
+    m = len(pl)
+    j = (pl.index(d) - pl.index(s)) % m
+    if 2 * j == m:
+        return 2 if 2 * widths[s] > max(widths) else pl.index(s) % 2
+    return 0 if 2 * j < m else 1
 
 
 def rank_program(g, core, T, topo):
     widths = T.tables["WIDTHS"]
     cores = T.cores
     n = len(cores)
-    base = core - core % 8
-    lane = core % 8
-    r = T.rank_of(base + RANK_LANE)
-    if r is None or (lane != RANK_LANE and lane not in HELPER):
+    me = core - core % 8 + RANK_LANE
+    mylane = core % 8
+    r = T.rank_of(me)
+    if r is None or mylane == 1:
         return
-    off = [sum(widths[:i]) for i in range(n)]
-
-    def piece(s, k):
-        h = widths[s] // 2
-        a = off[s] + k * h
-        return T.land[:, a:a + h]
-
-    def did(dst):
-        rid, pid = topo.addr(dst, core)
-        return DstId(rid=rid, pnc=pid)
-
-    def helper(s, k):
-        return cores[s] - RANK_LANE + HELPER[k]
-
-    def send(ap, dsts, mask, sem):
-        return RemoteDMATransfer(dst_ids=[did(d) for d in dsts], dma_engine_mask=mask, remote_sem=sem,
-                                 srcs=[ap], dsts=[ap for d in dsts])
-
-    me = cores[r]
-    peers = [s for s in range(n) if topo.same_plane(cores[s], me)]
+    off = [sum(widths[:i]) for i in range(n + 1)]
+    planes, lane, slot = plan(widths, cores, topo)
     mate = [s for s in range(n) if topo.mates(cores[s], me)][0]
     S = T.sem
+    sent = [0]
 
-    if lane == RANK_LANE:
-        g.dma_start(T.land[:, off[r]:off[r] + widths[r]], T.x[:, 0:widths[r]]).then_inc(S.ld, 16)
+    def on_chip_of(s, l):
+        return cores[s] - RANK_LANE + l
+
+    def cols(s, part):
+        w = widths[s]
+        a, b = ((0, w // 2), (w // 2, w), (0, w))[part]
+        return T.land[:, off[s] + a:off[s] + b]
+
+    def stage(s, part):
+        if part == 2:
+            return T["d%d" % widths[s]][slot[s]]
+        return T["h%d" % (widths[s] // 2)][part]
+
+    def tr(src, dst, to, mask, sem):
+        ids = []
+        for d in to:
+            rid, pid = topo.addr(d, core)
+            ids.append(DstId(rid=rid, pnc=pid))
+        sent[0] += bin(mask).count("1")
+        return RemoteDMATransfer(dst_ids=ids, dma_engine_mask=mask, remote_sem=sem, srcs=[src], dsts=[dst for d in to])
+
+    def parts(s, d):
+        return (0, 1) if s != d and way(s, d, planes, widths) == 2 else (2,)
+
+    blk = lambda s: S["blk%d" % slot[s]]
+    arr = lambda s: S["arr%d" % (s >= n // 2)]
+    split = any(way(r, d, planes, widths) == 2 for d in planes[r] if d != r)
+
+    if mylane == RANK_LANE:
+        g.sync.dma_start(cols(r, 2), T.x[:, 0:widths[r]]).then_inc(S.ld, 16)
         g.wait_ge(S.ld, 16)
-        g.remote_dma_fused([
-            send(piece(r, 0), [helper(s, 0) for s in peers + [r]], OFF, S.arr),
-            send(piece(r, 1), [helper(r, 1)], HI, S.own),
-        ], local_sem=S.sent)
-        g.wait_ge(S.sent, 16)
-        g.wait_ge(S.arr, 8 * (4 * len(peers) + 2))
-        g.dma_start(T.y[:, :], T.land[:, :]).then_inc(S.st, 16)
-        g.wait_ge(S.st, 16)
+        to = [on_chip_of(r, l) for l in DISTRIBUTOR + (lane[r],)]
+        g.remote_dma_fused([tr(cols(r, 2), stage(r, 2), to, ALL, blk(r))], local_sem=S.sent)
+        if split:
+            g.remote_dma_fused([tr(cols(r, k), stage(r, k), [on_chip_of(r, DISTRIBUTOR[k])], (OFF, HI)[k], S.half)
+                                for k in (0, 1)], local_sem=S.sent)
+        need = [0, 0]
+        for s in range(n):
+            if s != r:
+                need[s >= n // 2] += 8 * len(parts(s, r if s in planes[r] else mate))
+        for c, q in enumerate((g.sync, g.scalar)):
+            q.wait_ge(S["arr%d" % c], need[c])
+            if (r >= n // 2) == c:
+                q.wait_ge(S.ld, 16)
+            a, b = (0, off[n // 2], off[n])[c:c + 2]
+            q.dma_start(T.y[:, a:b], T.land[:, a:b]).then_inc(S.st, 16)
+        g.wait_ge(S.sent, sent[0])
+        g.wait_ge(S.st, 32)
         return
 
-    k = HELPER.index(lane)
-    sent = 0
-    if k == 1:
-        g.wait_ge(S.own, 8)
-        g.remote_dma_fused([send(piece(r, 1), [helper(s, 1) for s in peers] + [cores[mate]], OFF, S.arr)],
-                           local_sem=S.sent)
-        sent += 8
-        g.wait_ge(S.arr, 8 * len(peers))
-    else:
-        g.wait_ge(S.arr, 8 * (len(peers) + 1))
-        g.remote_dma_fused([send(piece(r, 0), [cores[mate]], OFF, S.arr)], local_sem=S.sent)
-        sent += 8
-    for s in peers:
-        g.remote_dma_fused([
-            send(piece(s, k), [cores[mate]], OFF, S.arr),
-            send(piece(s, k), [me], HI, S.arr),
-        ], local_sem=S.sent)
-        sent += 16
-    g.wait_ge(S.sent, sent)
+    if mylane in DISTRIBUTOR:
+        k = DISTRIBUTOR.index(mylane)
+        others = [d for d in planes[r] if d != r]
+        g.wait_ge(blk(r), 16)
+        to = [on_chip_of(d, lane[r]) for d in others if way(r, d, planes, widths) == k]
+        g.remote_dma_fused([tr(stage(r, 2), stage(r, 2), to, OFF, blk(r))], local_sem=S.sent)
+        if split:
+            g.wait_ge(S.half, 8)
+            to = [on_chip_of(d, lane[r]) for d in others if way(r, d, planes, widths) == 2]
+            g.remote_dma_fused([tr(stage(r, k), stage(r, k), to, OFF, blk(r))], local_sem=S.sent)
+        g.wait_ge(S.sent, sent[0])
+        return
+
+    for s in sorted([s for s in planes[r] if lane[s] == mylane], key=lambda s: slot[s]):
+        g.wait_ge(blk(s), 16 if s == r else 8 * len(parts(s, r)))
+        for p in parts(s, r):
+            trs = [tr(stage(s, p), cols(s, p), [cores[mate]], OFF, arr(s))]
+            if s != r:
+                trs.append(tr(stage(s, p), cols(s, p), [me], HI, arr(s)))
+            g.remote_dma_fused(trs, local_sem=S.sent)
+    g.wait_ge(S.sent, sent[0])

from concourse.bass import DstId, RemoteDMATransfer

SCRATCH = {
    "land": ("sbuf", [128, 3328], "float32"),
    "d256": ("dram", [2, 128, 256], "float32"),
    "d128": ("dram", [2, 128, 128], "float32"),
    "d64": ("dram", [2, 128, 64], "float32"),
    "h128": ("dram", [2, 128, 128], "float32"),
}
SEMAPHORES = ["ld", "st", "arr0", "arr1", "blk0", "blk1", "half", "sent"]

RANK_LANE = 5
DISTRIBUTOR = (4, 0)
FORWARDER = (6, 2, 3, 7)
ALL, OFF, HI = 0xFFFF, 0x00FF, 0xFF00


def plan(widths, cores, topo):
    n = len(cores)
    planes, lane, slot = {}, {}, {}
    for first in (0, 1):
        pl = [s for s in range(n) if s == first or topo.same_plane(cores[s], cores[first])]
        low = sorted([s for s in pl if s < n // 2], key=lambda s: -widths[s])
        high = sorted([s for s in pl if s >= n // 2], key=lambda s: widths[s])
        pairs = sorted(zip(low, high), key=lambda p: -(widths[p[0]] + widths[p[1]]))
        for i, p in enumerate(pairs):
            for j in (0, 1):
                lane[p[j]], slot[p[j]], planes[p[j]] = FORWARDER[i], j, pl
    return planes, lane, slot


def way(s, d, planes, widths):
    pl = planes[s]
    m = len(pl)
    j = (pl.index(d) - pl.index(s)) % m
    if 2 * j == m:
        return 2 if 2 * widths[s] > max(widths) else pl.index(s) % 2
    return 0 if 2 * j < m else 1


def rank_program(g, core, T, topo):
    widths = T.tables["WIDTHS"]
    cores = T.cores
    n = len(cores)
    me = core - core % 8 + RANK_LANE
    mylane = core % 8
    r = T.rank_of(me)
    if r is None or mylane == 1:
        return
    off = [sum(widths[:i]) for i in range(n + 1)]
    planes, lane, slot = plan(widths, cores, topo)
    mate = [s for s in range(n) if topo.mates(cores[s], me)][0]
    S = T.sem
    sent = [0]

    def on_chip_of(s, l):
        return cores[s] - RANK_LANE + l

    def cols(s, part):
        w = widths[s]
        a, b = ((0, w // 2), (w // 2, w), (0, w))[part]
        return T.land[:, off[s] + a:off[s] + b]

    def stage(s, part):
        if part == 2:
            return T["d%d" % widths[s]][slot[s]]
        return T["h%d" % (widths[s] // 2)][part]

    def tr(src, dst, to, mask, sem):
        ids = []
        for d in to:
            rid, pid = topo.addr(d, core)
            ids.append(DstId(rid=rid, pnc=pid))
        sent[0] += bin(mask).count("1")
        return RemoteDMATransfer(dst_ids=ids, dma_engine_mask=mask, remote_sem=sem, srcs=[src], dsts=[dst for d in to])

    def parts(s, d):
        return (0, 1) if s != d and way(s, d, planes, widths) == 2 else (2,)

    blk = lambda s: S["blk%d" % slot[s]]
    arr = lambda s: S["arr%d" % (s >= n // 2)]
    split = any(way(r, d, planes, widths) == 2 for d in planes[r] if d != r)

    if mylane == RANK_LANE:
        g.sync.dma_start(cols(r, 2), T.x[:, 0:widths[r]]).then_inc(S.ld, 16)
        g.wait_ge(S.ld, 16)
        to = [on_chip_of(r, l) for l in DISTRIBUTOR + (lane[r],)]
        g.remote_dma_fused([tr(cols(r, 2), stage(r, 2), to, ALL, blk(r))], local_sem=S.sent)
        if split:
            g.remote_dma_fused([tr(cols(r, k), stage(r, k), [on_chip_of(r, DISTRIBUTOR[k])], (OFF, HI)[k], S.half)
                                for k in (0, 1)], local_sem=S.sent)
        need = [0, 0]
        for s in range(n):
            if s != r:
                need[s >= n // 2] += 8 * len(parts(s, r if s in planes[r] else mate))
        for c, q in enumerate((g.sync, g.scalar)):
            q.wait_ge(S["arr%d" % c], need[c])
            if (r >= n // 2) == c:
                q.wait_ge(S.ld, 16)
            a, b = (0, off[n // 2], off[n])[c:c + 2]
            q.dma_start(T.y[:, a:b], T.land[:, a:b]).then_inc(S.st, 16)
        g.wait_ge(S.sent, sent[0])
        g.wait_ge(S.st, 32)
        return

    if mylane in DISTRIBUTOR:
        k = DISTRIBUTOR.index(mylane)
        others = [d for d in planes[r] if d != r]
        g.wait_ge(blk(r), 16)
        to = [on_chip_of(d, lane[r]) for d in others if way(r, d, planes, widths) == k]
        g.remote_dma_fused([tr(stage(r, 2), stage(r, 2), to, OFF, blk(r))], local_sem=S.sent)
        if split:
            g.wait_ge(S.half, 8)
            to = [on_chip_of(d, lane[r]) for d in others if way(r, d, planes, widths) == 2]
            g.remote_dma_fused([tr(stage(r, k), stage(r, k), to, OFF, blk(r))], local_sem=S.sent)
        g.wait_ge(S.sent, sent[0])
        return

    for s in sorted([s for s in planes[r] if lane[s] == mylane], key=lambda s: slot[s]):
        g.wait_ge(blk(s), 16 if s == r else 8 * len(parts(s, r)))
        for p in parts(s, r):
            trs = [tr(stage(s, p), cols(s, p), [cores[mate]], OFF, arr(s))]
            if s != r:
                trs.append(tr(stage(s, p), cols(s, p), [me], HI, arr(s)))
            g.remote_dma_fused(trs, local_sem=S.sent)
    g.wait_ge(S.sent, sent[0])
